import numpy as np, ml_dtypes
CORES = [1,17,65,89,97,113]
N = 6
QP = 64
def setup_inputs(rng):
    m = 150 * rng.standard_normal((1, QP, 1), dtype=np.float32) + 3 * rng.standard_normal((N, QP, 1), dtype=np.float32)
    m = (m + rng.uniform(100, 300, (1, QP, 1)) * (rng.random((1, QP, 1)) < 0.7) * (rng.random((N, QP, 1)) < 0.5)).astype(np.float32)
    l = 20 * (1 + np.abs(rng.standard_normal((N, QP, 1), dtype=np.float32)))
    return {"o": (l * rng.standard_normal((N, QP, 128), dtype=np.float32) / 4).astype(ml_dtypes.bfloat16), "ml": np.concatenate([m, l], axis=2)}
def setup_inputs_big(rng):
    d = setup_inputs(rng)
    for k in ("o",): d[k] = (d[k].astype(np.float32) * 1048576.0).astype(d[k].dtype)
    return d
def setup_inputs_small(rng):
    d = setup_inputs(rng)
    for k in ("o",): d[k] = (d[k].astype(np.float32) * (1 / 1048576.0)).astype(d[k].dtype)
    return d
def setup_inputs_apart(rng):
    d = setup_inputs(rng)
    f = (10.0 ** rng.permutation(np.linspace(-1.5, 1.5, N))).astype(np.float32).reshape(N, 1, 1)
    for k in ("o",): d[k] = (d[k].astype(np.float32) * f).astype(d[k].dtype)
    return d
def reference(o, ml):
    O, ML = o.astype(np.float64), ml.astype(np.float64)
    m, l = ML[:, :, 0:1], ML[:, :, 1:2]
    f = np.exp(m - m.max(axis=0))
    y = ((f * O).sum(axis=0) / (f * l).sum(axis=0)).astype(ml_dtypes.bfloat16)
    return {"y": np.broadcast_to(y, (N,) + y.shape)}

@@ -1,0 +1,253 @@
+from concourse.bass import DstId, RemoteDMATransfer
+from concourse.mybir import AluOpType, AxisListType, ActivationFunctionType
+
+SLOT = 72
+C_LO, C_HI, C_L, C_O = 5, 6, 7, 8
+PW = SLOT - C_LO
+NPOOL = 34
+
+SCRATCH = {
+    "land": ("sbuf", [128, 6, SLOT], "bfloat16"),
+    "relay": ("sbuf", [128, PW], "bfloat16"),
+    "mlsb": ("sbuf", [128, 2], "float32"),
+    "ones": ("sbuf", [128, 128], "bfloat16"),
+    "ident": ("sbuf", [128, 128], "bfloat16"),
+    "diag": ("sbuf", [128, 7, 128], "bfloat16"),
+    "nm1": ("sbuf", [128, 8], "float32"),
+    "nm2": ("sbuf", [128, 8], "float32"),
+    "na": ("sbuf", [128, 1], "float32"),
+    "nc": ("sbuf", [128, 1], "bfloat16"),
+    "wc": ("sbuf", [128, 1], "float32"),
+    "cc": ("sbuf", [128, 1], "bfloat16"),
+    "f1": ("sbuf", [128, 8], "float32"),
+    "f2": ("sbuf", [128, 8], "float32"),
+    "part": ("sbuf", [128, 65], "bfloat16"),
+    "rc": ("sbuf", [128, 1], "float32"),
+    "ysb": ("sbuf", [128, 64], "bfloat16"),
+    "ps1": ("psum", [128, 512], "float32"),
+    "ps2": ("psum", [128, 512], "float32"),
+}
+SEMAPHORES = (["ldml", "ldo", "ones", "ident", "rin", "sent", "st"] + ["f%d" % i for i in range(6)]
+              + ["c%d" % i for i in range(NPOOL)])
+
+ADD, SUB, MUL = AluOpType.add, AluOpType.subtract, AluOpType.mult
+MIN, MAX = AluOpType.min, AluOpType.max
+EXP, COPY = ActivationFunctionType.Exp, ActivationFunctionType.Copy
+
+
+def _bits(mask):
+    return bin(mask).count("1")
+
+
+def _plan(cores, topo):
+    n = len(cores)
+    direct, relays, helpers = {}, {}, {}
+    for i, ci in enumerate(cores):
+        ring = [(i + d) % n for d in range(1, n)]
+        direct[i] = [k for k in ring if topo.may_write(ci, cores[k])]
+        far = [k for k in ring if not topo.may_write(ci, cores[k])]
+        helpers[i] = []
+        if far:
+            cand = [c for c in range(topo.CHIPS * topo.CORES_PER_CHIP)
+                    if topo.chip(c) == topo.chip(ci) and c not in cores
+                    and all(topo.may_write(c, cores[k]) for k in far)]
+            cand.sort(key=lambda c: (topo.die(c) != topo.die(ci), c))
+            nh = 1 if len(far) < 2 else 2
+            cut = (len(far) + nh - 1) // nh
+            for h in range(nh):
+                relays[cand[h]] = (i, far[h * cut:(h + 1) * cut])
+                helpers[i].append(cand[h])
+    order = {}
+    for k in range(n):
+        early = sorted([i for i in range(n) if k in direct[i]], key=lambda i: direct[i].index(k))
+        late = [i for i in range(n) if i != k and k not in direct[i]]
+        order[k] = (early, late)
+    return direct, relays, helpers, order
+
+
+def _slot(order, k, i):
+    early, late = order[k]
+    return 1 + (early + late).index(i)
+
+
+def _send(g, T, topo, core, src, dests, aps, sem):
+    mask = topo.mask(core, dests[0])
+    for d in dests:
+        mask &= topo.mask(core, d)
+    for c in T.cores:
+        if c != core:
+            mask &= topo.mask(core, c)
+    ids = []
+    for d in dests:
+        rid, pid, _se = topo.addr(d)
+        ids.append(DstId(rid=rid, pnc=pid))
+    g.remote_dma_fused([RemoteDMATransfer(dst_ids=ids, dma_engine_mask=mask, remote_sem=sem, srcs=[src], dsts=aps)],
+                       local_sem=T.sem.sent)
+    return _bits(mask)
+
+
+def rank_program(g, core, T, topo):
+    cores = list(T.cores)
+    direct, relays, helpers, order = _plan(cores, topo)
+    S = T.sem
+    land = T.land
+
+    if core in relays:
+        i, dests = relays[core]
+        nin = _bits(topo.mask(cores[i], core) & topo.mask(cores[i], cores[dests[0]]))
+        g.wait_ge(S.rin, nin)
+        n = _send(g, T, topo, core, T.relay[:, :], [cores[k] for k in dests],
+                  [land[:, _slot(order, k, i), C_LO:SLOT] for k in dests], S["f%d" % i])
+        g.wait_ge(S.sent, n)
+        return
+
+    rank = T.rank_of(core)
+    if rank is None:
+        return
+    v, a, pe, sy = g.vector, g.scalar, g.tensor, g.sync
+    pool = [0]
+
+    def sem():
+        pool[0] += 1
+        return S["c%d" % (pool[0] - 1)]
+
+    early, late = order[rank]
+    others = early + late
+    NE = _bits(topo.mask(core, cores[others[0]]))
+
+    v.memset(T.ones[:, :], 1.0).then_inc(S.ones, 1)
+    sy.dma_start(T.mlsb[0:64, :], T.ml[:, :]).then_inc(S.ldml, 16)
+    a.dma_start(T.mlsb[64:128, :], T.ml[:, :]).then_inc(S.ldml, 16)
+    sy.dma_start(land[0:64, 0, C_O:SLOT], T.o[:, 0:64]).then_inc(S.ldo, 16)
+    a.dma_start(land[64:128, 0, C_O:SLOT], T.o[:, 64:128]).then_inc(S.ldo, 16)
+    g.wait_ge(S.ones, 1)
+    g.affine_select(T.ident[:, :], T.ones[:, :], [[-1, 128]], AluOpType.is_equal, 0.0, 0, 1).then_inc(S.ident, 1)
+
+    pa, pb, pc = sem(), sem(), sem()
+    v.wait_ge(S.ldml, 32)
+    v.tensor_scalar(land[:, 0, C_HI:C_HI + 1], T.mlsb[:, 0:1], -1.0, None, MUL).then_inc(pa, 1)
+    v.wait_ge(pa, 1)
+    v.tensor_scalar(land[:, 0, C_LO:C_LO + 1], T.mlsb[:, 0:1], -1.0, land[:, 0, C_HI:C_HI + 1], MUL, SUB).then_inc(pc, 1)
+    a.wait_ge(S.ldml, 32)
+    a.activation(land[:, 0, C_L:C_L + 1], T.mlsb[:, 1:2], COPY).then_inc(pb, 1)
+
+    g.wait_ge(S.ldo, 32)
+    g.wait_ge(pa, 1)
+    g.wait_ge(pb, 1)
+    g.wait_ge(pc, 1)
+    src = land[:, 0, C_LO:SLOT]
+    nsent = 0
+    if helpers[rank]:
+        nsent += _send(g, T, topo, core, src, helpers[rank], [T.relay[:, :] for _h in helpers[rank]], S.rin)
+    if direct[rank]:
+        nsent += _send(g, T, topo, core, src, [cores[k] for k in direct[rank]],
+                       [land[:, _slot(order, k, rank), C_LO:SLOT] for k in direct[rank]], S["f%d" % rank])
+
+    for q in (v, a):
+        q.wait_ge(S.ident, 1)
+    pe.wait_ge(S.ldo, 32)
+    pe.wait_ge(pb, 1)
+    v.wait_ge(pc, 1)
+
+    def weighted(ps, fcol, rhs, waits, dslot, first, last):
+        ins = None
+        ds = []
+        for e in range(len(rhs)):
+            d = sem()
+            ds.append(d)
+            if e % 2 == 0:
+                v.tensor_scalar(T.diag[:, dslot + e, :], T.ident[:, :], fcol[e], None, MUL).then_inc(d, 1)
+            else:
+                a.activation(T.diag[:, dslot + e, :], T.ident[:, :], COPY, scale=fcol[e]).then_inc(d, 1)
+        for e in range(len(rhs)):
+            pe.wait_ge(ds[e], 1)
+            for (s, n) in waits[e]:
+                pe.wait_ge(s, n)
+            ins = pe.matmul(ps, T.diag[:, dslot + e, :], rhs[e], first and e == 0, last and e == len(rhs) - 1)
+        return ins
+
+    def arr(i):
+        return (S["f%d" % i], NE)
+
+    if len(late) == 1 and len(early) >= 2:
+        ps = T.ps2[:, 0:65]
+        s1, s2, s3, m1, p1 = sem(), sem(), sem(), sem(), sem()
+        v.wait_ge(*arr(early[0]))
+        v.tensor_tensor(T.nm1[:, 0:2], land[:, 0:2, C_HI], land[:, 0:2, C_LO], ADD).then_inc(s1, 1)
+        v.wait_ge(s1, 1)
+        v.tensor_reduce(T.nm2[:, 0:1], T.nm1[:, 0:2], AxisListType.X, MIN).then_inc(s2, 1)
+        a.wait_ge(s1, 1)
+        a.wait_ge(s2, 1)
+        a.activation(T.f1[:, 0:2], T.nm1[:, 0:2], EXP, bias=T.nm2[:, 0:1], scale=-1.0).then_inc(s3, 1)
+        v.wait_ge(s3, 1)
+        a.wait_ge(s3, 1)
+        weighted(T.ps1[:, 0:65], [T.f1[:, e:e + 1] for e in range(2)], [land[:, e, C_L:SLOT] for e in range(2)],
+                 [[], [arr(early[0])]], 0, True, True).then_inc(m1, 1)
+        v.wait_ge(m1, 1)
+        v.tensor_copy(T.part[:, :], T.ps1[:, 0:65]).then_inc(p1, 1)
+        k = len(early)
+        s5, s6, s6b, s7 = sem(), sem(), sem(), sem()
+        for i in early[1:]:
+            v.wait_ge(*arr(i))
+        v.wait_ge(s2, 1)
+        v.tensor_tensor(T.nm2[:, 1:k], land[:, 2:k + 1, C_HI], land[:, 2:k + 1, C_LO], ADD).then_inc(s5, 1)
+        v.wait_ge(s5, 1)
+        v.tensor_reduce(T.na[:, 0:1], T.nm2[:, 0:k], AxisListType.X, MIN).then_inc(s6, 1)
+        v.wait_ge(s6, 1)
+        v.tensor_scalar(T.nc[:, 0:1], T.na[:, 0:1], -60.0, None, ADD).then_inc(s6b, 1)
+        a.wait_ge(s5, 1)
+        a.wait_ge(s6, 1)
+        a.activation(T.f2[:, 0:k], T.nm2[:, 0:k], EXP, bias=T.na[:, 0:1], scale=-1.0).then_inc(s7, 1)
+        v.wait_ge(s7, 1)
+        a.wait_ge(s7, 1)
+        weighted(ps, [T.f2[:, e:e + 1] for e in range(k)],
+                 [T.part[:, :]] + [land[:, e + 1, C_L:SLOT] for e in range(1, k)],
+                 [[(p1, 1)]] + [[arr(i)] for i in early[1:]], 2, True, False)
+        s8, s9, s10 = sem(), sem(), sem()
+        ls = k + 1
+        v.wait_ge(*arr(late[0]))
+        v.wait_ge(s6b, 1)
+        v.tensor_scalar(T.wc[:, 0:1], land[:, ls, C_HI:C_HI + 1], land[:, ls, C_LO:C_LO + 1], T.nc[:, 0:1],
+                        ADD, MAX).then_inc(s8, 1)
+        a.wait_ge(s8, 1)
+        a.activation(T.cc[:, 0:1], T.wc[:, 0:1], EXP, bias=T.na[:, 0:1], scale=-1.0).then_inc(s9, 1)
+        v.wait_ge(s9, 1)
+        v.tensor_scalar(T.diag[:, 6, :], T.ident[:, :], T.cc[:, 0:1], None, MUL).then_inc(s10, 1)
+        pe.wait_ge(s10, 1)
+        pe.wait_ge(*arr(late[0]))
+        mm = pe.matmul(ps, T.diag[:, 6, :], land[:, ls, C_L:SLOT], False, True)
+    else:
+        ps = T.ps2[:, 0:65]
+        k = 1 + len(others)
+        s1, s2, s3 = sem(), sem(), sem()
+        for i in others:
+            v.wait_ge(*arr(i))
+        v.tensor_tensor(T.nm1[:, 0:k], land[:, 0:k, C_HI], land[:, 0:k, C_LO], ADD).then_inc(s1, 1)
+        v.wait_ge(s1, 1)
+        v.tensor_reduce(T.na[:, 0:1], T.nm1[:, 0:k], AxisListType.X, MIN).then_inc(s2, 1)
+        v.wait_ge(s2, 1)
+        v.tensor_scalar(T.f1[:, 0:k], T.nm1[:, 0:k], T.na[:, 0:1], -1.0 / 128.0, SUB, MUL).then_inc(s3, 1)
+        v.wait_ge(s3, 1)
+        sq = sem()
+        v.tensor_scalar(T.f2[:, 0:k], T.f1[:, 0:k], 1.0, 0.0, ADD, MAX).then_inc(sq, 1)
+        for _t in range(7):
+            v.wait_ge(sq, 1)
+            sq = sem()
+            v.tensor_tensor(T.f2[:, 0:k], T.f2[:, 0:k], T.f2[:, 0:k], MUL).then_inc(sq, 1)
+        v.wait_ge(sq, 1)
+        a.wait_ge(sq, 1)
+        mm = weighted(ps, [T.f2[:, e:e + 1] for e in range(k)], [land[:, e, C_L:SLOT] for e in range(k)],
+                      [[]] + [[arr(i)] for i in others], 0, True, True)
+
+    m2, s11, s12 = sem(), sem(), sem()
+    mm.then_inc(m2, 1)
+    v.wait_ge(m2, 1)
+    v.reciprocal(T.rc[:, 0:1], T.ps2[:, 0:1]).then_inc(s11, 1)
+    v.wait_ge(s11, 1)
+    v.tensor_scalar(T.ysb[:, :], T.ps2[:, 1:65], T.rc[:, 0:1], None, MUL).then_inc(s12, 1)
+    sy.wait_ge(s12, 1)
+    sy.dma_start(T.y[:, 0:64], T.ysb[0:64, :]).then_inc(S.st, 16)
+    a.wait_ge(s12, 1)
+    a.dma_start(T.y[:, 64:128], T.ysb[64:128, :]).then_inc(S.st, 16)
+    g.wait_ge(S.sent, nsent)
+    g.wait_ge(S.st, 32)

@@ -4,7 +4,7 @@ from concourse.mybir import AluOpType, AxisListType, ActivationFunctionType
 SLOT = 72
 C_LO, C_HI, C_L, C_O = 5, 6, 7, 8
 PW = SLOT - C_LO
-NPOOL = 34
+NPOOL = 26
 
 SCRATCH = {
     "land": ("sbuf", [128, 6, SLOT], "bfloat16"),
@@ -12,20 +12,18 @@ SCRATCH = {
     "mlsb": ("sbuf", [128, 2], "float32"),
     "ones": ("sbuf", [128, 128], "bfloat16"),
     "ident": ("sbuf", [128, 128], "bfloat16"),
-    "diag": ("sbuf", [128, 7, 128], "bfloat16"),
-    "nm1": ("sbuf", [128, 8], "float32"),
-    "nm2": ("sbuf", [128, 8], "float32"),
+    "sc": ("sbuf", [128, 7, SLOT], "bfloat16"),
+    "nm": ("sbuf", [128, 8], "float32"),
     "na": ("sbuf", [128, 1], "float32"),
     "nc": ("sbuf", [128, 1], "bfloat16"),
     "wc": ("sbuf", [128, 1], "float32"),
     "cc": ("sbuf", [128, 1], "bfloat16"),
+    "f0": ("sbuf", [128, 1], "float32"),
     "f1": ("sbuf", [128, 8], "float32"),
-    "f2": ("sbuf", [128, 8], "float32"),
     "part": ("sbuf", [128, 65], "bfloat16"),
     "rc": ("sbuf", [128, 1], "float32"),
     "ysb": ("sbuf", [128, 64], "bfloat16"),
-    "ps1": ("psum", [128, 512], "float32"),
-    "ps2": ("psum", [128, 512], "float32"),
+    "ps": ("psum", [128, 512], "float32"),
 }
 SEMAPHORES = (["ldml", "ldo", "ones", "ident", "rin", "sent", "st"] + ["f%d" % i for i in range(6)]
               + ["c%d" % i for i in range(NPOOL)])
@@ -115,6 +113,9 @@ def rank_program(g, core, T, topo):
     others = early + late
     NE = _bits(topo.mask(core, cores[others[0]]))
 
+    def arr(i):
+        return (S["f%d" % i], NE)
+
     v.memset(T.ones[:, :], 1.0).then_inc(S.ones, 1)
     sy.dma_start(T.mlsb[0:64, :], T.ml[:, :]).then_inc(S.ldml, 16)
     a.dma_start(T.mlsb[64:128, :], T.ml[:, :]).then_inc(S.ldml, 16)
@@ -143,108 +144,70 @@ def rank_program(g, core, T, topo):
         nsent += _send(g, T, topo, core, src, [cores[k] for k in direct[rank]],
                        [land[:, _slot(order, k, rank), C_LO:SLOT] for k in direct[rank]], S["f%d" % rank])
 
-    for q in (v, a):
-        q.wait_ge(S.ident, 1)
-    pe.wait_ge(S.ldo, 32)
-    pe.wait_ge(pb, 1)
+    z1, z2, z3 = sem(), sem(), sem()
     v.wait_ge(pc, 1)
+    v.tensor_tensor(T.nm[:, 0:1], land[:, 0, C_HI:C_HI + 1], land[:, 0, C_LO:C_LO + 1], ADD).then_inc(z1, 1)
+    a.wait_ge(z1, 1)
+    a.activation(T.f0[:, 0:1], T.nm[:, 0:1], EXP, bias=T.nm[:, 0:1], scale=-1.0).then_inc(z2, 1)
+    v.wait_ge(z2, 1)
+    v.wait_ge(S.ldo, 32)
+    v.wait_ge(pb, 1)
+    v.tensor_scalar(T.part[:, :], land[:, 0, C_L:SLOT], T.f0[:, 0:1], None, MUL).then_inc(z3, 1)
+    v.wait_ge(z1, 1)
+    v.wait_ge(z3, 1)
+    pe.wait_ge(S.ident, 1)
 
-    def weighted(ps, fcol, rhs, waits, dslot, first, last):
-        ins = None
-        ds = []
-        for e in range(len(rhs)):
-            d = sem()
-            ds.append(d)
-            if e % 2 == 0:
-                v.tensor_scalar(T.diag[:, dslot + e, :], T.ident[:, :], fcol[e], None, MUL).then_inc(d, 1)
-            else:
-                a.activation(T.diag[:, dslot + e, :], T.ident[:, :], COPY, scale=fcol[e]).then_inc(d, 1)
-        for e in range(len(rhs)):
-            pe.wait_ge(ds[e], 1)
-            for (s, n) in waits[e]:
-                pe.wait_ge(s, n)
-            ins = pe.matmul(ps, T.diag[:, dslot + e, :], rhs[e], first and e == 0, last and e == len(rhs) - 1)
-        return ins
+    ratio = len(late) == 1 and len(early) >= 1
+    now = early if ratio else others
+    k = 1 + len(now)
+    ps = T.ps[:, 0:65]
+    s5, s6, s7 = sem(), sem(), sem()
+    for i in now:
+        v.wait_ge(*arr(i))
+        a.wait_ge(*arr(i))
+    v.tensor_tensor(T.nm[:, 1:k], land[:, 1:k, C_HI], land[:, 1:k, C_LO], ADD).then_inc(s5, 1)
+    v.wait_ge(s5, 1)
+    v.tensor_reduce(T.na[:, 0:1], T.nm[:, 0:k], AxisListType.X, MIN).then_inc(s6, 1)
+    a.wait_ge(s5, 1)
+    a.wait_ge(s6, 1)
+    a.activation(T.f1[:, 0:k], T.nm[:, 0:k], EXP, bias=T.na[:, 0:1], scale=-1.0).then_inc(s7, 1)
+    v.wait_ge(s7, 1)
+    a.wait_ge(s7, 1)
+    ds = []
+    for e in range(k):
+        d = sem()
+        ds.append(d)
+        x = T.part[:, :] if e == 0 else land[:, e, C_L:SLOT]
+        if e % 2 == 0:
+            v.tensor_scalar(T.sc[:, e, 0:65], x, T.f1[:, e:e + 1], None, MUL).then_inc(d, 1)
+        else:
+            a.activation(T.sc[:, e, 0:65], x, COPY, scale=T.f1[:, e:e + 1]).then_inc(d, 1)
+    mm = None
+    for e in range(k):
+        pe.wait_ge(ds[e], 1)
+        mm = pe.matmul(ps, T.ident[:, :], T.sc[:, e, 0:65], e == 0, (not ratio) and e == k - 1)
 
-    def arr(i):
-        return (S["f%d" % i], NE)
-
-    if len(late) == 1 and len(early) >= 2:
-        ps = T.ps2[:, 0:65]
-        s1, s2, s3, m1, p1 = sem(), sem(), sem(), sem(), sem()
-        v.wait_ge(*arr(early[0]))
-        v.tensor_tensor(T.nm1[:, 0:2], land[:, 0:2, C_HI], land[:, 0:2, C_LO], ADD).then_inc(s1, 1)
-        v.wait_ge(s1, 1)
-        v.tensor_reduce(T.nm2[:, 0:1], T.nm1[:, 0:2], AxisListType.X, MIN).then_inc(s2, 1)
-        a.wait_ge(s1, 1)
-        a.wait_ge(s2, 1)
-        a.activation(T.f1[:, 0:2], T.nm1[:, 0:2], EXP, bias=T.nm2[:, 0:1], scale=-1.0).then_inc(s3, 1)
-        v.wait_ge(s3, 1)
-        a.wait_ge(s3, 1)
-        weighted(T.ps1[:, 0:65], [T.f1[:, e:e + 1] for e in range(2)], [land[:, e, C_L:SLOT] for e in range(2)],
-                 [[], [arr(early[0])]], 0, True, True).then_inc(m1, 1)
-        v.wait_ge(m1, 1)
-        v.tensor_copy(T.part[:, :], T.ps1[:, 0:65]).then_inc(p1, 1)
-        k = len(early)
-        s5, s6, s6b, s7 = sem(), sem(), sem(), sem()
-        for i in early[1:]:
-            v.wait_ge(*arr(i))
-        v.wait_ge(s2, 1)
-        v.tensor_tensor(T.nm2[:, 1:k], land[:, 2:k + 1, C_HI], land[:, 2:k + 1, C_LO], ADD).then_inc(s5, 1)
-        v.wait_ge(s5, 1)
-        v.tensor_reduce(T.na[:, 0:1], T.nm2[:, 0:k], AxisListType.X, MIN).then_inc(s6, 1)
+    if ratio:
+        s6b, s8, s9, s10 = sem(), sem(), sem(), sem()
         v.wait_ge(s6, 1)
         v.tensor_scalar(T.nc[:, 0:1], T.na[:, 0:1], -60.0, None, ADD).then_inc(s6b, 1)
-        a.wait_ge(s5, 1)
-        a.wait_ge(s6, 1)
-        a.activation(T.f2[:, 0:k], T.nm2[:, 0:k], EXP, bias=T.na[:, 0:1], scale=-1.0).then_inc(s7, 1)
-        v.wait_ge(s7, 1)
-        a.wait_ge(s7, 1)
-        weighted(ps, [T.f2[:, e:e + 1] for e in range(k)],
-                 [T.part[:, :]] + [land[:, e + 1, C_L:SLOT] for e in range(1, k)],
-                 [[(p1, 1)]] + [[arr(i)] for i in early[1:]], 2, True, False)
-        s8, s9, s10 = sem(), sem(), sem()
-        ls = k + 1
-        v.wait_ge(*arr(late[0]))
         v.wait_ge(s6b, 1)
-        v.tensor_scalar(T.wc[:, 0:1], land[:, ls, C_HI:C_HI + 1], land[:, ls, C_LO:C_LO + 1], T.nc[:, 0:1],
+        v.wait_ge(*arr(late[0]))
+        v.tensor_scalar(T.wc[:, 0:1], land[:, k, C_HI:C_HI + 1], land[:, k, C_LO:C_LO + 1], T.nc[:, 0:1],
                         ADD, MAX).then_inc(s8, 1)
         a.wait_ge(s8, 1)
         a.activation(T.cc[:, 0:1], T.wc[:, 0:1], EXP, bias=T.na[:, 0:1], scale=-1.0).then_inc(s9, 1)
         v.wait_ge(s9, 1)
-        v.tensor_scalar(T.diag[:, 6, :], T.ident[:, :], T.cc[:, 0:1], None, MUL).then_inc(s10, 1)
+        v.tensor_scalar(T.sc[:, k, 0:65], land[:, k, C_L:SLOT], T.cc[:, 0:1], None, MUL).then_inc(s10, 1)
         pe.wait_ge(s10, 1)
-        pe.wait_ge(*arr(late[0]))
-        mm = pe.matmul(ps, T.diag[:, 6, :], land[:, ls, C_L:SLOT], False, True)
-    else:
-        ps = T.ps2[:, 0:65]
-        k = 1 + len(others)
-        s1, s2, s3 = sem(), sem(), sem()
-        for i in others:
-            v.wait_ge(*arr(i))
-        v.tensor_tensor(T.nm1[:, 0:k], land[:, 0:k, C_HI], land[:, 0:k, C_LO], ADD).then_inc(s1, 1)
-        v.wait_ge(s1, 1)
-        v.tensor_reduce(T.na[:, 0:1], T.nm1[:, 0:k], AxisListType.X, MIN).then_inc(s2, 1)
-        v.wait_ge(s2, 1)
-        v.tensor_scalar(T.f1[:, 0:k], T.nm1[:, 0:k], T.na[:, 0:1], -1.0 / 128.0, SUB, MUL).then_inc(s3, 1)
-        v.wait_ge(s3, 1)
-        sq = sem()
-        v.tensor_scalar(T.f2[:, 0:k], T.f1[:, 0:k], 1.0, 0.0, ADD, MAX).then_inc(sq, 1)
-        for _t in range(7):
-            v.wait_ge(sq, 1)
-            sq = sem()
-            v.tensor_tensor(T.f2[:, 0:k], T.f2[:, 0:k], T.f2[:, 0:k], MUL).then_inc(sq, 1)
-        v.wait_ge(sq, 1)
-        a.wait_ge(sq, 1)
-        mm = weighted(ps, [T.f2[:, e:e + 1] for e in range(k)], [land[:, e, C_L:SLOT] for e in range(k)],
-                      [[]] + [[arr(i)] for i in others], 0, True, True)
+        mm = pe.matmul(ps, T.ident[:, :], T.sc[:, k, 0:65], False, True)
 
     m2, s11, s12 = sem(), sem(), sem()
     mm.then_inc(m2, 1)
     v.wait_ge(m2, 1)
-    v.reciprocal(T.rc[:, 0:1], T.ps2[:, 0:1]).then_inc(s11, 1)
+    v.reciprocal(T.rc[:, 0:1], T.ps[:, 0:1]).then_inc(s11, 1)
     v.wait_ge(s11, 1)
-    v.tensor_scalar(T.ysb[:, :], T.ps2[:, 1:65], T.rc[:, 0:1], None, MUL).then_inc(s12, 1)
+    v.tensor_scalar(T.ysb[:, :], T.ps[:, 1:65], T.rc[:, 0:1], None, MUL).then_inc(s12, 1)
     sy.wait_ge(s12, 1)
     sy.dma_start(T.y[:, 0:64], T.ysb[0:64, :]).then_inc(S.st, 16)
     a.wait_ge(s12, 1)

@@ -2,14 +2,16 @@ from concourse.bass import DstId, RemoteDMATransfer
 from concourse.mybir import AluOpType, AxisListType, ActivationFunctionType
 
 SLOT = 72
-C_LO, C_HI, C_L, C_O = 5, 6, 7, 8
-PW = SLOT - C_LO
-NPOOL = 26
+C_HI, C_LO, C_L, C_O = 5, 6, 7, 8
+PW = SLOT - C_HI
+NPOOL = 28
+BIG = 100663296.0
 
 SCRATCH = {
     "land": ("sbuf", [128, 6, SLOT], "bfloat16"),
     "relay": ("sbuf", [128, PW], "bfloat16"),
-    "mlsb": ("sbuf", [128, 2], "float32"),
+    "x": ("sbuf", [128, 12], "float32"),
+    "yc": ("sbuf", [128, 4], "float32"),
     "ones": ("sbuf", [128, 128], "bfloat16"),
     "ident": ("sbuf", [128, 128], "bfloat16"),
     "sc": ("sbuf", [128, 7, SLOT], "bfloat16"),
@@ -17,15 +19,17 @@ SCRATCH = {
     "na": ("sbuf", [128, 1], "float32"),
     "nc": ("sbuf", [128, 1], "bfloat16"),
     "wc": ("sbuf", [128, 1], "float32"),
-    "cc": ("sbuf", [128, 1], "bfloat16"),
+    "cc": ("sbuf", [128, 1], "float32"),
+    "dn": ("sbuf", [128, 1], "float32"),
     "f0": ("sbuf", [128, 1], "float32"),
     "f1": ("sbuf", [128, 8], "float32"),
     "part": ("sbuf", [128, 65], "bfloat16"),
     "rc": ("sbuf", [128, 1], "float32"),
     "ysb": ("sbuf", [128, 64], "bfloat16"),
     "ps": ("psum", [128, 512], "float32"),
+    "psd": ("psum", [128, 512], "float32"),
 }
-SEMAPHORES = (["ldml", "ldo", "ones", "ident", "rin", "sent", "st"] + ["f%d" % i for i in range(6)]
+SEMAPHORES = (["ldml", "ldo", "ones", "cst", "ident", "rin", "sent", "st"] + ["f%d" % i for i in range(6)]
               + ["c%d" % i for i in range(NPOOL)])
 
 ADD, SUB, MUL = AluOpType.add, AluOpType.subtract, AluOpType.mult
@@ -40,6 +44,7 @@ def _bits(mask):
 def _plan(cores, topo):
     n = len(cores)
     direct, relays, helpers = {}, {}, {}
+    load = {}
     for i, ci in enumerate(cores):
         ring = [(i + d) % n for d in range(1, n)]
         direct[i] = [k for k in ring if topo.may_write(ci, cores[k])]
@@ -49,12 +54,26 @@ def _plan(cores, topo):
             cand = [c for c in range(topo.CHIPS * topo.CORES_PER_CHIP)
                     if topo.chip(c) == topo.chip(ci) and c not in cores
                     and all(topo.may_write(c, cores[k]) for k in far)]
-            cand.sort(key=lambda c: (topo.die(c) != topo.die(ci), c))
             nh = 1 if len(far) < 2 else 2
             cut = (len(far) + nh - 1) // nh
             for h in range(nh):
-                relays[cand[h]] = (i, far[h * cut:(h + 1) * cut])
-                helpers[i].append(cand[h])
+                chunk = far[h * cut:(h + 1) * cut]
+
+                def cost(c):
+                    d = topo.die(c)
+                    busy = load.get(("out", topo.chip(c), d), 0)
+                    for k in chunk:
+                        busy += load.get(("in", topo.chip(cores[k]), d), 0)
+                    return (busy, d != topo.die(ci), c)
+
+                c = min([c for c in cand if c not in relays], key=cost)
+                d = topo.die(c)
+                load[("out", topo.chip(c), d)] = load.get(("out", topo.chip(c), d), 0) + len(chunk)
+                for k in chunk:
+                    key = ("in", topo.chip(cores[k]), d)
+                    load[key] = load.get(key, 0) + 1
+                relays[c] = (i, chunk)
+                helpers[i].append(c)
     order = {}
     for k in range(n):
         early = sorted([i for i in range(n) if k in direct[i]], key=lambda i: direct[i].index(k))
@@ -68,13 +87,16 @@ def _slot(order, k, i):
     return 1 + (early + late).index(i)
 
 
-def _send(g, T, topo, core, src, dests, aps, sem):
+def _mask(T, topo, core, dests):
     mask = topo.mask(core, dests[0])
-    for d in dests:
-        mask &= topo.mask(core, d)
-    for c in T.cores:
+    for c in list(dests) + list(T.cores):
         if c != core:
             mask &= topo.mask(core, c)
+    return mask
+
+
+def _send(g, T, topo, core, src, dests, aps, sem):
+    mask = _mask(T, topo, core, dests)
     ids = []
     for d in dests:
         rid, pid, _se = topo.addr(d)
@@ -92,10 +114,9 @@ def rank_program(g, core, T, topo):
 
     if core in relays:
         i, dests = relays[core]
-        nin = _bits(topo.mask(cores[i], core) & topo.mask(cores[i], cores[dests[0]]))
-        g.wait_ge(S.rin, nin)
+        g.wait_ge(S.rin, _bits(_mask(T, topo, cores[i], [core])))
         n = _send(g, T, topo, core, T.relay[:, :], [cores[k] for k in dests],
-                  [land[:, _slot(order, k, i), C_LO:SLOT] for k in dests], S["f%d" % i])
+                  [land[:, _slot(order, k, i), C_HI:SLOT] for k in dests], S["f%d" % i])
         g.wait_ge(S.sent, n)
         return
 
@@ -116,37 +137,40 @@ def rank_program(g, core, T, topo):
     def arr(i):
         return (S["f%d" % i], NE)
 
-    v.memset(T.ones[:, :], 1.0).then_inc(S.ones, 1)
-    sy.dma_start(T.mlsb[0:64, :], T.ml[:, :]).then_inc(S.ldml, 16)
-    a.dma_start(T.mlsb[64:128, :], T.ml[:, :]).then_inc(S.ldml, 16)
+    sy.dma_start(T.x[0:64, 8:10], T.ml[:, :]).then_inc(S.ldml, 16)
+    a.dma_start(T.x[64:128, 8:10], T.ml[:, :]).then_inc(S.ldml, 16)
     sy.dma_start(land[0:64, 0, C_O:SLOT], T.o[:, 0:64]).then_inc(S.ldo, 16)
     a.dma_start(land[64:128, 0, C_O:SLOT], T.o[:, 64:128]).then_inc(S.ldo, 16)
+    v.memset(T.ones[:, :], 1.0).then_inc(S.ones, 1)
+    v.memset(T.x[:, 0:1], BIG).then_inc(S.cst, 1)
+    v.memset(T.x[:, 4:5], -BIG).then_inc(S.cst, 1)
+    v.memset(T.yc[:, 0:1], 1.0).then_inc(S.cst, 1)
+    v.memset(T.yc[:, 1:2], -1.0).then_inc(S.cst, 1)
+    v.memset(T.yc[:, 2:3], 1.0).then_inc(S.cst, 1)
     g.wait_ge(S.ones, 1)
     g.affine_select(T.ident[:, :], T.ones[:, :], [[-1, 128]], AluOpType.is_equal, 0.0, 0, 1).then_inc(S.ident, 1)
 
-    pa, pb, pc = sem(), sem(), sem()
+    pb, pc = sem(), sem()
+    v.wait_ge(S.cst, 5)
     v.wait_ge(S.ldml, 32)
-    v.tensor_scalar(land[:, 0, C_HI:C_HI + 1], T.mlsb[:, 0:1], -1.0, None, MUL).then_inc(pa, 1)
-    v.wait_ge(pa, 1)
-    v.tensor_scalar(land[:, 0, C_LO:C_LO + 1], T.mlsb[:, 0:1], -1.0, land[:, 0, C_HI:C_HI + 1], MUL, SUB).then_inc(pc, 1)
+    v.tensor_tensor_scan(land[:, 0, C_HI - 1:C_LO + 1], T.x[:, 0:12:4], T.yc[:, 0:3], T.x[:, 8:9], ADD, MUL).then_inc(pc, 1)
     a.wait_ge(S.ldml, 32)
-    a.activation(land[:, 0, C_L:C_L + 1], T.mlsb[:, 1:2], COPY).then_inc(pb, 1)
+    a.activation(land[:, 0, C_L:C_L + 1], T.x[:, 9:10], COPY).then_inc(pb, 1)
 
     g.wait_ge(S.ldo, 32)
-    g.wait_ge(pa, 1)
     g.wait_ge(pb, 1)
     g.wait_ge(pc, 1)
-    src = land[:, 0, C_LO:SLOT]
+    src = land[:, 0, C_HI:SLOT]
     nsent = 0
     if helpers[rank]:
         nsent += _send(g, T, topo, core, src, helpers[rank], [T.relay[:, :] for _h in helpers[rank]], S.rin)
     if direct[rank]:
         nsent += _send(g, T, topo, core, src, [cores[k] for k in direct[rank]],
-                       [land[:, _slot(order, k, rank), C_LO:SLOT] for k in direct[rank]], S["f%d" % rank])
+                       [land[:, _slot(order, k, rank), C_HI:SLOT] for k in direct[rank]], S["f%d" % rank])
 
     z1, z2, z3 = sem(), sem(), sem()
     v.wait_ge(pc, 1)
-    v.tensor_tensor(T.nm[:, 0:1], land[:, 0, C_HI:C_HI + 1], land[:, 0, C_LO:C_LO + 1], ADD).then_inc(z1, 1)
+    v.tensor_tensor(T.nm[:, 0:1], land[:, 0, C_HI:C_HI + 1], land[:, 0, C_LO:C_LO + 1], SUB).then_inc(z1, 1)
     a.wait_ge(z1, 1)
     a.activation(T.f0[:, 0:1], T.nm[:, 0:1], EXP, bias=T.nm[:, 0:1], scale=-1.0).then_inc(z2, 1)
     v.wait_ge(z2, 1)
@@ -165,9 +189,8 @@ def rank_program(g, core, T, topo):
     for i in now:
         v.wait_ge(*arr(i))
         a.wait_ge(*arr(i))
-    v.tensor_tensor(T.nm[:, 1:k], land[:, 1:k, C_HI], land[:, 1:k, C_LO], ADD).then_inc(s5, 1)
-    v.wait_ge(s5, 1)
-    v.tensor_reduce(T.na[:, 0:1], T.nm[:, 0:k], AxisListType.X, MIN).then_inc(s6, 1)
+    v.tensor_reduce(T.na[:, 0:1], land[:, 0:k, C_HI], AxisListType.X, MIN).then_inc(s6, 1)
+    v.tensor_tensor(T.nm[:, 1:k], land[:, 1:k, C_HI], land[:, 1:k, C_LO], SUB).then_inc(s5, 1)
     a.wait_ge(s5, 1)
     a.wait_ge(s6, 1)
     a.activation(T.f1[:, 0:k], T.nm[:, 0:k], EXP, bias=T.na[:, 0:1], scale=-1.0).then_inc(s7, 1)
@@ -183,29 +206,42 @@ def rank_program(g, core, T, topo):
         else:
             a.activation(T.sc[:, e, 0:65], x, COPY, scale=T.f1[:, e:e + 1]).then_inc(d, 1)
     mm = None
+    md = None
     for e in range(k):
         pe.wait_ge(ds[e], 1)
         mm = pe.matmul(ps, T.ident[:, :], T.sc[:, e, 0:65], e == 0, (not ratio) and e == k - 1)
+        if ratio:
+            md = pe.matmul(T.psd[:, 0:1], T.ident[:, :], T.sc[:, e, 0:1], e == 0, e == k - 1)
 
+    m2, s11, s12 = sem(), sem(), sem()
     if ratio:
-        s6b, s8, s9, s10 = sem(), sem(), sem(), sem()
+        s6b, s8, s9, s10, sd, sn = sem(), sem(), sem(), sem(), sem(), sem()
+        md.then_inc(sd, 1)
         v.wait_ge(s6, 1)
         v.tensor_scalar(T.nc[:, 0:1], T.na[:, 0:1], -60.0, None, ADD).then_inc(s6b, 1)
         v.wait_ge(s6b, 1)
+        v.wait_ge(sd, 1)
         v.wait_ge(*arr(late[0]))
         v.tensor_scalar(T.wc[:, 0:1], land[:, k, C_HI:C_HI + 1], land[:, k, C_LO:C_LO + 1], T.nc[:, 0:1],
-                        ADD, MAX).then_inc(s8, 1)
+                        SUB, MAX).then_inc(s8, 1)
+        a.wait_ge(*arr(late[0]))
         a.wait_ge(s8, 1)
         a.activation(T.cc[:, 0:1], T.wc[:, 0:1], EXP, bias=T.na[:, 0:1], scale=-1.0).then_inc(s9, 1)
-        v.wait_ge(s9, 1)
-        v.tensor_scalar(T.sc[:, k, 0:65], land[:, k, C_L:SLOT], T.cc[:, 0:1], None, MUL).then_inc(s10, 1)
+        a.wait_ge(s9, 1)
+        a.activation(T.sc[:, k, 0:65], land[:, k, C_L:SLOT], COPY, scale=T.cc[:, 0:1]).then_inc(s10, 1)
         pe.wait_ge(s10, 1)
         mm = pe.matmul(ps, T.ident[:, :], T.sc[:, k, 0:65], False, True)
+        v.wait_ge(s9, 1)
+        v.tensor_scalar(T.dn[:, 0:1], land[:, k, C_L:C_L + 1], T.cc[:, 0:1], T.psd[:, 0:1], MUL, ADD).then_inc(sn, 1)
+        v.wait_ge(sn, 1)
+        v.reciprocal(T.rc[:, 0:1], T.dn[:, 0:1]).then_inc(s11, 1)
+        mm.then_inc(m2, 1)
+        v.wait_ge(m2, 1)
+    else:
+        mm.then_inc(m2, 1)
+        v.wait_ge(m2, 1)
+        v.reciprocal(T.rc[:, 0:1], T.ps[:, 0:1]).then_inc(s11, 1)
 
-    m2, s11, s12 = sem(), sem(), sem()
-    mm.then_inc(m2, 1)
-    v.wait_ge(m2, 1)
-    v.reciprocal(T.rc[:, 0:1], T.ps[:, 0:1]).then_inc(s11, 1)
     v.wait_ge(s11, 1)
     v.tensor_scalar(T.ysb[:, :], T.ps[:, 1:65], T.rc[:, 0:1], None, MUL).then_inc(s12, 1)
     sy.wait_ge(s12, 1)

@@ -29,7 +29,7 @@ SCRATCH = {
     "ps": ("psum", [128, 512], "float32"),
     "psd": ("psum", [128, 512], "float32"),
 }
-SEMAPHORES = (["ldml", "ldo", "ones", "cst", "ident", "rin", "sent", "st"] + ["f%d" % i for i in range(6)]
+SEMAPHORES = (["ldml", "ldo", "ones", "cst", "ident", "idin", "rin", "sent", "st"] + ["f%d" % i for i in range(6)]
               + ["c%d" % i for i in range(NPOOL)])
 
 ADD, SUB, MUL = AluOpType.add, AluOpType.subtract, AluOpType.mult
@@ -114,9 +114,16 @@ def rank_program(g, core, T, topo):
 
     if core in relays:
         i, dests = relays[core]
+        w = 128 // len(helpers[i])
+        c0 = w * helpers[i].index(core)
+        g.vector.memset(T.ones[:, 0:w], 1.0).then_inc(S.ones, 1)
+        g.wait_ge(S.ones, 1)
+        g.affine_select(T.ident[:, c0:c0 + w], T.ones[:, 0:w], [[-1, w]], AluOpType.is_equal, 0.0, -c0, 1).then_inc(S.ident, 1)
+        g.wait_ge(S.ident, 1)
+        n = _send(g, T, topo, core, T.ident[:, c0:c0 + w], [cores[i]], [T.ident[:, c0:c0 + w]], S.idin)
         g.wait_ge(S.rin, _bits(_mask(T, topo, cores[i], [core])))
-        n = _send(g, T, topo, core, T.relay[:, :], [cores[k] for k in dests],
-                  [land[:, _slot(order, k, i), C_HI:SLOT] for k in dests], S["f%d" % i])
+        n += _send(g, T, topo, core, T.relay[:, :], [cores[k] for k in dests],
+                   [land[:, _slot(order, k, i), C_HI:SLOT] for k in dests], S["f%d" % i])
         g.wait_ge(S.sent, n)
         return
 
@@ -141,14 +148,16 @@ def rank_program(g, core, T, topo):
     a.dma_start(T.x[64:128, 8:10], T.ml[:, :]).then_inc(S.ldml, 16)
     sy.dma_start(land[0:64, 0, C_O:SLOT], T.o[:, 0:64]).then_inc(S.ldo, 16)
     a.dma_start(land[64:128, 0, C_O:SLOT], T.o[:, 64:128]).then_inc(S.ldo, 16)
-    v.memset(T.ones[:, :], 1.0).then_inc(S.ones, 1)
+    if not helpers[rank]:
+        v.memset(T.ones[:, :], 1.0).then_inc(S.ones, 1)
     v.memset(T.x[:, 0:1], BIG).then_inc(S.cst, 1)
     v.memset(T.x[:, 4:5], -BIG).then_inc(S.cst, 1)
     v.memset(T.yc[:, 0:1], 1.0).then_inc(S.cst, 1)
     v.memset(T.yc[:, 1:2], -1.0).then_inc(S.cst, 1)
     v.memset(T.yc[:, 2:3], 1.0).then_inc(S.cst, 1)
-    g.wait_ge(S.ones, 1)
-    g.affine_select(T.ident[:, :], T.ones[:, :], [[-1, 128]], AluOpType.is_equal, 0.0, 0, 1).then_inc(S.ident, 1)
+    if not helpers[rank]:
+        g.wait_ge(S.ones, 1)
+        g.affine_select(T.ident[:, :], T.ones[:, :], [[-1, 128]], AluOpType.is_equal, 0.0, 0, 1).then_inc(S.ident, 1)
 
     pb, pc = sem(), sem()
     v.wait_ge(S.cst, 5)
@@ -179,7 +188,10 @@ def rank_program(g, core, T, topo):
     v.tensor_scalar(T.part[:, :], land[:, 0, C_L:SLOT], T.f0[:, 0:1], None, MUL).then_inc(z3, 1)
     v.wait_ge(z1, 1)
     v.wait_ge(z3, 1)
-    pe.wait_ge(S.ident, 1)
+    if helpers[rank]:
+        pe.wait_ge(S.idin, sum(_bits(_mask(T, topo, h, [core])) for h in helpers[rank]))
+    else:
+        pe.wait_ge(S.ident, 1)
 
     ratio = len(late) == 1 and len(early) >= 1
     now = early if ratio else others

@@ -4,7 +4,8 @@ from concourse.mybir import AluOpType, AxisListType, ActivationFunctionType
 SLOT = 72
 C_HI, C_LO, C_L, C_O = 5, 6, 7, 8
 PW = SLOT - C_HI
-NPOOL = 28
+NPOOL = 30
+BW = 8
 BIG = 100663296.0
 
 SCRATCH = {
@@ -13,6 +14,9 @@ SCRATCH = {
     "x": ("sbuf", [128, 12], "float32"),
     "yc": ("sbuf", [128, 4], "float32"),
     "ones": ("sbuf", [128, 128], "bfloat16"),
+    "blk": ("sbuf", [128, BW], "bfloat16"),
+    "zc": ("sbuf", [128, 1], "float32"),
+    "fl": ("sbuf", [128, 8], "float32"),
     "ident": ("sbuf", [128, 128], "bfloat16"),
     "sc": ("sbuf", [128, 7, SLOT], "bfloat16"),
     "nm": ("sbuf", [128, 8], "float32"),
@@ -29,8 +33,8 @@ SCRATCH = {
     "ps": ("psum", [128, 512], "float32"),
     "psd": ("psum", [128, 512], "float32"),
 }
-SEMAPHORES = (["ldml", "ldo", "ones", "cst", "ident", "idin", "rin", "sent", "st"] + ["f%d" % i for i in range(6)]
-              + ["c%d" % i for i in range(NPOOL)])
+SEMAPHORES = (["ldml", "ldo", "ones", "cst", "zc", "ident", "blk", "bin", "idin", "rin", "sent", "st"]
+              + ["f%d" % i for i in range(6)] + ["c%d" % i for i in range(NPOOL)])
 
 ADD, SUB, MUL = AluOpType.add, AluOpType.subtract, AluOpType.mult
 MIN, MAX = AluOpType.min, AluOpType.max
@@ -74,12 +78,24 @@ def _plan(cores, topo):
                     load[key] = load.get(key, 0) + 1
                 relays[c] = (i, chunk)
                 helpers[i].append(c)
+    carry, carriers, makers = {}, {}, {}
+    for i, ci in enumerate(cores):
+        carriers[i] = []
+        for h in helpers[i]:
+            chunk = relays[h][1]
+            free = [c for c in range(topo.CHIPS * topo.CORES_PER_CHIP)
+                    if topo.chip(c) == topo.chip(ci) and c not in cores and c not in relays and c not in carry
+                    and all(topo.may_write(c, cores[k]) for k in chunk)]
+            c = min(free, key=lambda c: (topo.die(c) != topo.die(h), c)) if free else h
+            carry[c] = (i, chunk)
+            carriers[i].append(c)
+        makers[i] = helpers[i] + [c for c in carriers[i] if c not in helpers[i]]
     order = {}
     for k in range(n):
         early = sorted([i for i in range(n) if k in direct[i]], key=lambda i: direct[i].index(k))
         late = [i for i in range(n) if i != k and k not in direct[i]]
         order[k] = (early, late)
-    return direct, relays, helpers, order
+    return direct, relays, helpers, carry, carriers, makers, order
 
 
 def _slot(order, k, i):
@@ -87,16 +103,30 @@ def _slot(order, k, i):
     return 1 + (early + late).index(i)
 
 
-def _mask(T, topo, core, dests):
+def _idcols(order, makers, k, h):
+    base = BW * len(order[k][1])
+    rest = 128 - base
+    nh = len(makers[k])
+    return base + rest * h // nh, base + rest * (h + 1) // nh
+
+
+def _blkcol(order, carry, carriers, i):
+    pos = sorted({order[k][1].index(i) for c in carriers[i] for k in carry[c][1]})
+    if len(pos) != 1:
+        raise ValueError("rank %d: its block would stand at unlike columns" % i)
+    return BW * pos[0]
+
+
+def _mask(T, topo, core, dests, wide=False):
     mask = topo.mask(core, dests[0])
-    for c in list(dests) + list(T.cores):
+    for c in list(dests) + ([] if wide else list(T.cores)):
         if c != core:
             mask &= topo.mask(core, c)
     return mask
 
 
-def _send(g, T, topo, core, src, dests, aps, sem):
-    mask = _mask(T, topo, core, dests)
+def _send(g, T, topo, core, src, dests, aps, sem, wide=False):
+    mask = _mask(T, topo, core, dests, wide)
     ids = []
     for d in dests:
         rid, pid, _se = topo.addr(d)
@@ -108,22 +138,30 @@ def _send(g, T, topo, core, src, dests, aps, sem):
 
 def rank_program(g, core, T, topo):
     cores = list(T.cores)
-    direct, relays, helpers, order = _plan(cores, topo)
+    direct, relays, helpers, carry, carriers, makers, order = _plan(cores, topo)
     S = T.sem
     land = T.land
 
-    if core in relays:
-        i, dests = relays[core]
-        w = 128 // len(helpers[i])
-        c0 = w * helpers[i].index(core)
+    if core in relays or core in carry:
+        i = relays[core][0] if core in relays else carry[core][0]
+        lo, hi = _idcols(order, makers, i, makers[i].index(core))
+        w = hi - lo
         g.vector.memset(T.ones[:, 0:w], 1.0).then_inc(S.ones, 1)
         g.wait_ge(S.ones, 1)
-        g.affine_select(T.ident[:, c0:c0 + w], T.ones[:, 0:w], [[-1, w]], AluOpType.is_equal, 0.0, -c0, 1).then_inc(S.ident, 1)
+        g.affine_select(T.ident[:, lo:hi], T.ones[:, 0:w], [[-1, w]], AluOpType.is_equal, 0.0, -lo, 1).then_inc(S.ident, 1)
         g.wait_ge(S.ident, 1)
-        n = _send(g, T, topo, core, T.ident[:, c0:c0 + w], [cores[i]], [T.ident[:, c0:c0 + w]], S.idin)
-        g.wait_ge(S.rin, _bits(_mask(T, topo, cores[i], [core])))
-        n += _send(g, T, topo, core, T.relay[:, :], [cores[k] for k in dests],
-                   [land[:, _slot(order, k, i), C_HI:SLOT] for k in dests], S["f%d" % i])
+        n = _send(g, T, topo, core, T.ident[:, lo:hi], [cores[i]], [T.ident[:, lo:hi]], S.idin)
+        if core in carry:
+            dests = carry[core][1]
+            b0 = _blkcol(order, carry, carriers, i)
+            g.wait_ge(S.bin, _bits(_mask(T, topo, cores[i], [core], True)))
+            n += _send(g, T, topo, core, T.blk[:, :], [cores[k] for k in dests],
+                       [T.ident[:, b0:b0 + BW] for _k in dests], S.idin)
+        if core in relays:
+            dests = relays[core][1]
+            g.wait_ge(S.rin, _bits(_mask(T, topo, cores[i], [core], True)))
+            n += _send(g, T, topo, core, T.relay[:, :], [cores[k] for k in dests],
+                       [land[:, _slot(order, k, i), C_HI:SLOT] for k in dests], S["f%d" % i])
         g.wait_ge(S.sent, n)
         return
 
@@ -148,49 +186,60 @@ def rank_program(g, core, T, topo):
     a.dma_start(T.x[64:128, 8:10], T.ml[:, :]).then_inc(S.ldml, 16)
     sy.dma_start(land[0:64, 0, C_O:SLOT], T.o[:, 0:64]).then_inc(S.ldo, 16)
     a.dma_start(land[64:128, 0, C_O:SLOT], T.o[:, 64:128]).then_inc(S.ldo, 16)
-    if not helpers[rank]:
-        v.memset(T.ones[:, :], 1.0).then_inc(S.ones, 1)
+    base = BW * len(late)
+    nsent = 0
+    v.memset(T.ones[:, 0:(BW if helpers[rank] else 128 - base)], 1.0).then_inc(S.ones, 1)
+    v.memset(T.zc[:, 0:1], 0.0).then_inc(S.zc, 1)
     v.memset(T.x[:, 0:1], BIG).then_inc(S.cst, 1)
     v.memset(T.x[:, 4:5], -BIG).then_inc(S.cst, 1)
     v.memset(T.yc[:, 0:1], 1.0).then_inc(S.cst, 1)
     v.memset(T.yc[:, 1:2], -1.0).then_inc(S.cst, 1)
     v.memset(T.yc[:, 2:3], 1.0).then_inc(S.cst, 1)
-    if not helpers[rank]:
-        g.wait_ge(S.ones, 1)
-        g.affine_select(T.ident[:, :], T.ones[:, :], [[-1, 128]], AluOpType.is_equal, 0.0, 0, 1).then_inc(S.ident, 1)
+    g.wait_ge(S.ones, 1)
+    if helpers[rank]:
+        b0 = _blkcol(order, carry, carriers, rank)
+        g.affine_select(T.blk[:, :], T.ones[:, 0:BW], [[-1, BW]], AluOpType.is_equal, 0.0, -b0, 1).then_inc(S.blk, 1)
+        g.wait_ge(S.blk, 1)
+        nsent += _send(g, T, topo, core, T.blk[:, :], carriers[rank], [T.blk[:, :] for _h in carriers[rank]], S.bin, True)
+    else:
+        g.affine_select(T.ident[:, base:128], T.ones[:, 0:128 - base], [[-1, 128 - base]], AluOpType.is_equal, 0.0,
+                        -base, 1).then_inc(S.ident, 1)
+    z2 = sem()
+    a.wait_ge(S.zc, 1)
+    a.activation(T.f0[:, 0:1], T.zc[:, 0:1], EXP).then_inc(z2, 1)
 
     pb, pc = sem(), sem()
     v.wait_ge(S.cst, 5)
     v.wait_ge(S.ldml, 32)
     v.tensor_tensor_scan(land[:, 0, C_HI - 1:C_LO + 1], T.x[:, 0:12:4], T.yc[:, 0:3], T.x[:, 8:9], ADD, MUL).then_inc(pc, 1)
-    a.wait_ge(S.ldml, 32)
-    a.activation(land[:, 0, C_L:C_L + 1], T.x[:, 9:10], COPY).then_inc(pb, 1)
+    v.tensor_copy(land[:, 0, C_L:C_L + 1], T.x[:, 9:10]).then_inc(pb, 1)
 
     g.wait_ge(S.ldo, 32)
     g.wait_ge(pb, 1)
     g.wait_ge(pc, 1)
     src = land[:, 0, C_HI:SLOT]
-    nsent = 0
     if helpers[rank]:
-        nsent += _send(g, T, topo, core, src, helpers[rank], [T.relay[:, :] for _h in helpers[rank]], S.rin)
+        nsent += _send(g, T, topo, core, src, helpers[rank], [T.relay[:, :] for _h in helpers[rank]], S.rin, True)
     if direct[rank]:
         nsent += _send(g, T, topo, core, src, [cores[k] for k in direct[rank]],
                        [land[:, _slot(order, k, rank), C_HI:SLOT] for k in direct[rank]], S["f%d" % rank])
 
-    z1, z2, z3 = sem(), sem(), sem()
+    z1, z3 = sem(), sem()
     v.wait_ge(pc, 1)
     v.tensor_tensor(T.nm[:, 0:1], land[:, 0, C_HI:C_HI + 1], land[:, 0, C_LO:C_LO + 1], SUB).then_inc(z1, 1)
-    a.wait_ge(z1, 1)
-    a.activation(T.f0[:, 0:1], T.nm[:, 0:1], EXP, bias=T.nm[:, 0:1], scale=-1.0).then_inc(z2, 1)
     v.wait_ge(z2, 1)
     v.wait_ge(S.ldo, 32)
     v.wait_ge(pb, 1)
     v.tensor_scalar(T.part[:, :], land[:, 0, C_L:SLOT], T.f0[:, 0:1], None, MUL).then_inc(z3, 1)
     v.wait_ge(z1, 1)
     v.wait_ge(z3, 1)
-    if helpers[rank]:
-        pe.wait_ge(S.idin, sum(_bits(_mask(T, topo, h, [core])) for h in helpers[rank]))
-    else:
+    a.wait_ge(z1, 1)
+    nid = sum(_bits(_mask(T, topo, h, [core])) for h in makers[rank])
+    for i in late:
+        nid += sum(_bits(_mask(T, topo, c, [core])) for c in carriers[i] if rank in carry[c][1])
+    if nid:
+        pe.wait_ge(S.idin, nid)
+    if not helpers[rank]:
         pe.wait_ge(S.ident, 1)
 
     ratio = len(late) == 1 and len(early) >= 1
@@ -203,6 +252,10 @@ def rank_program(g, core, T, topo):
         a.wait_ge(*arr(i))
     v.tensor_reduce(T.na[:, 0:1], land[:, 0:k, C_HI], AxisListType.X, MIN).then_inc(s6, 1)
     v.tensor_tensor(T.nm[:, 1:k], land[:, 1:k, C_HI], land[:, 1:k, C_LO], SUB).then_inc(s5, 1)
+    s6b = sem()
+    if ratio:
+        v.wait_ge(s6, 1)
+        v.tensor_scalar(T.nc[:, 0:1], T.na[:, 0:1], -60.0, None, ADD).then_inc(s6b, 1)
     a.wait_ge(s5, 1)
     a.wait_ge(s6, 1)
     a.activation(T.f1[:, 0:k], T.nm[:, 0:k], EXP, bias=T.na[:, 0:1], scale=-1.0).then_inc(s7, 1)
@@ -213,7 +266,7 @@ def rank_program(g, core, T, topo):
         d = sem()
         ds.append(d)
         x = T.part[:, :] if e == 0 else land[:, e, C_L:SLOT]
-        if e % 2 == 0:
+        if (e % 2 == 0) if ratio else (e == 0):
             v.tensor_scalar(T.sc[:, e, 0:65], x, T.f1[:, e:e + 1], None, MUL).then_inc(d, 1)
         else:
             a.activation(T.sc[:, e, 0:65], x, COPY, scale=T.f1[:, e:e + 1]).then_inc(d, 1)
@@ -227,12 +280,9 @@ def rank_program(g, core, T, topo):
 
     m2, s11, s12 = sem(), sem(), sem()
     if ratio:
-        s6b, s8, s9, s10, sd, sn = sem(), sem(), sem(), sem(), sem(), sem()
+        s8, s9, s10, sd, sn = sem(), sem(), sem(), sem(), sem()
         md.then_inc(sd, 1)
-        v.wait_ge(s6, 1)
-        v.tensor_scalar(T.nc[:, 0:1], T.na[:, 0:1], -60.0, None, ADD).then_inc(s6b, 1)
         v.wait_ge(s6b, 1)
-        v.wait_ge(sd, 1)
         v.wait_ge(*arr(late[0]))
         v.tensor_scalar(T.wc[:, 0:1], land[:, k, C_HI:C_HI + 1], land[:, k, C_LO:C_LO + 1], T.nc[:, 0:1],
                         SUB, MAX).then_inc(s8, 1)
@@ -244,15 +294,21 @@ def rank_program(g, core, T, topo):
         pe.wait_ge(s10, 1)
         mm = pe.matmul(ps, T.ident[:, :], T.sc[:, k, 0:65], False, True)
         v.wait_ge(s9, 1)
+        v.wait_ge(sd, 1)
         v.tensor_scalar(T.dn[:, 0:1], land[:, k, C_L:C_L + 1], T.cc[:, 0:1], T.psd[:, 0:1], MUL, ADD).then_inc(sn, 1)
         v.wait_ge(sn, 1)
         v.reciprocal(T.rc[:, 0:1], T.dn[:, 0:1]).then_inc(s11, 1)
         mm.then_inc(m2, 1)
         v.wait_ge(m2, 1)
     else:
+        sa, sb = sem(), sem()
+        v.tensor_tensor(T.fl[:, 0:k], T.f1[:, 0:k], land[:, 0:k, C_L], MUL).then_inc(sa, 1)
+        v.wait_ge(sa, 1)
+        v.tensor_reduce(T.dn[:, 0:1], T.fl[:, 0:k], AxisListType.X, ADD).then_inc(sb, 1)
+        v.wait_ge(sb, 1)
+        v.reciprocal(T.rc[:, 0:1], T.dn[:, 0:1]).then_inc(s11, 1)
         mm.then_inc(m2, 1)
         v.wait_ge(m2, 1)
-        v.reciprocal(T.rc[:, 0:1], T.ps[:, 0:1]).then_inc(s11, 1)
 
     v.wait_ge(s11, 1)
     v.tensor_scalar(T.ysb[:, :], T.ps[:, 1:65], T.rc[:, 0:1], None, MUL).then_inc(s12, 1)

from concourse.bass import DstId, RemoteDMATransfer
from concourse.mybir import AluOpType, AxisListType, ActivationFunctionType

SLOT = 72
C_HI, C_LO, C_L, C_O = 5, 6, 7, 8
PW = SLOT - C_HI
NPOOL = 30
BW = 8
BIG = 100663296.0

SCRATCH = {
    "land": ("sbuf", [128, 6, SLOT], "bfloat16"),
    "relay": ("sbuf", [128, PW], "bfloat16"),
    "x": ("sbuf", [128, 12], "float32"),
    "yc": ("sbuf", [128, 4], "float32"),
    "ones": ("sbuf", [128, 128], "bfloat16"),
    "blk": ("sbuf", [128, BW], "bfloat16"),
    "zc": ("sbuf", [128, 1], "float32"),
    "fl": ("sbuf", [128, 8], "float32"),
    "ident": ("sbuf", [128, 128], "bfloat16"),
    "sc": ("sbuf", [128, 7, SLOT], "bfloat16"),
    "nm": ("sbuf", [128, 8], "float32"),
    "na": ("sbuf", [128, 1], "float32"),
    "nc": ("sbuf", [128, 1], "bfloat16"),
    "wc": ("sbuf", [128, 1], "float32"),
    "cc": ("sbuf", [128, 1], "float32"),
    "dn": ("sbuf", [128, 1], "float32"),
    "f0": ("sbuf", [128, 1], "float32"),
    "f1": ("sbuf", [128, 8], "float32"),
    "part": ("sbuf", [128, 65], "bfloat16"),
    "rc": ("sbuf", [128, 1], "float32"),
    "ysb": ("sbuf", [128, 64], "bfloat16"),
    "ps": ("psum", [128, 512], "float32"),
    "psd": ("psum", [128, 512], "float32"),
}
SEMAPHORES = (["ldml", "ldo", "ones", "cst", "zc", "ident", "blk", "bin", "idin", "rin", "sent", "st"]
              + ["f%d" % i for i in range(6)] + ["c%d" % i for i in range(NPOOL)])

ADD, SUB, MUL = AluOpType.add, AluOpType.subtract, AluOpType.mult
MIN, MAX = AluOpType.min, AluOpType.max
EXP, COPY = ActivationFunctionType.Exp, ActivationFunctionType.Copy


def _bits(mask):
    return bin(mask).count("1")


def _plan(cores, topo):
    n = len(cores)
    direct, relays, helpers = {}, {}, {}
    load = {}
    for i, ci in enumerate(cores):
        ring = [(i + d) % n for d in range(1, n)]
        direct[i] = [k for k in ring if topo.may_write(ci, cores[k])]
        far = [k for k in ring if not topo.may_write(ci, cores[k])]
        helpers[i] = []
        if far:
            cand = [c for c in range(topo.CHIPS * topo.CORES_PER_CHIP)
                    if topo.chip(c) == topo.chip(ci) and c not in cores
                    and all(topo.may_write(c, cores[k]) for k in far)]
            nh = 1 if len(far) < 2 else 2
            cut = (len(far) + nh - 1) // nh
            for h in range(nh):
                chunk = far[h * cut:(h + 1) * cut]

                def cost(c):
                    d = topo.die(c)
                    busy = load.get(("out", topo.chip(c), d), 0)
                    for k in chunk:
                        busy += load.get(("in", topo.chip(cores[k]), d), 0)
                    return (busy, d != topo.die(ci), c)

                c = min([c for c in cand if c not in relays], key=cost)
                d = topo.die(c)
                load[("out", topo.chip(c), d)] = load.get(("out", topo.chip(c), d), 0) + len(chunk)
                for k in chunk:
                    key = ("in", topo.chip(cores[k]), d)
                    load[key] = load.get(key, 0) + 1
                relays[c] = (i, chunk)
                helpers[i].append(c)
    carry, carriers, makers = {}, {}, {}
    for i, ci in enumerate(cores):
        carriers[i] = []
        for h in helpers[i]:
            chunk = relays[h][1]
            free = [c for c in range(topo.CHIPS * topo.CORES_PER_CHIP)
                    if topo.chip(c) == topo.chip(ci) and c not in cores and c not in relays and c not in carry
                    and all(topo.may_write(c, cores[k]) for k in chunk)]
            c = min(free, key=lambda c: (topo.die(c) != topo.die(h), c)) if free else h
            carry[c] = (i, chunk)
            carriers[i].append(c)
        makers[i] = helpers[i] + [c for c in carriers[i] if c not in helpers[i]]
    order = {}
    for k in range(n):
        early = sorted([i for i in range(n) if k in direct[i]], key=lambda i: direct[i].index(k))
        late = [i for i in range(n) if i != k and k not in direct[i]]
        order[k] = (early, late)
    return direct, relays, helpers, carry, carriers, makers, order


def _slot(order, k, i):
    early, late = order[k]
    return 1 + (early + late).index(i)


def _idcols(order, makers, k, h):
    base = BW * len(order[k][1])
    rest = 128 - base
    nh = len(makers[k])
    return base + rest * h // nh, base + rest * (h + 1) // nh


def _blkcol(order, carry, carriers, i):
    pos = sorted({order[k][1].index(i) for c in carriers[i] for k in carry[c][1]})
    if len(pos) != 1:
        raise ValueError("rank %d: its block would stand at unlike columns" % i)
    return BW * pos[0]


def _mask(T, topo, core, dests, wide=False):
    mask = topo.mask(core, dests[0])
    for c in list(dests) + ([] if wide else list(T.cores)):
        if c != core:
            mask &= topo.mask(core, c)
    return mask


def _send(g, T, topo, core, src, dests, aps, sem, wide=False):
    mask = _mask(T, topo, core, dests, wide)
    ids = []
    for d in dests:
        rid, pid, _se = topo.addr(d)
        ids.append(DstId(rid=rid, pnc=pid))
    g.remote_dma_fused([RemoteDMATransfer(dst_ids=ids, dma_engine_mask=mask, remote_sem=sem, srcs=[src], dsts=aps)],
                       local_sem=T.sem.sent)
    return _bits(mask)


def rank_program(g, core, T, topo):
    cores = list(T.cores)
    direct, relays, helpers, carry, carriers, makers, order = _plan(cores, topo)
    S = T.sem
    land = T.land

    if core in relays or core in carry:
        i = relays[core][0] if core in relays else carry[core][0]
        lo, hi = _idcols(order, makers, i, makers[i].index(core))
        w = hi - lo
        g.vector.memset(T.ones[:, 0:w], 1.0).then_inc(S.ones, 1)
        g.wait_ge(S.ones, 1)
        g.affine_select(T.ident[:, lo:hi], T.ones[:, 0:w], [[-1, w]], AluOpType.is_equal, 0.0, -lo, 1).then_inc(S.ident, 1)
        g.wait_ge(S.ident, 1)
        n = _send(g, T, topo, core, T.ident[:, lo:hi], [cores[i]], [T.ident[:, lo:hi]], S.idin)
        if core in carry:
            dests = carry[core][1]
            b0 = _blkcol(order, carry, carriers, i)
            g.wait_ge(S.bin, _bits(_mask(T, topo, cores[i], [core], True)))
            n += _send(g, T, topo, core, T.blk[:, :], [cores[k] for k in dests],
                       [T.ident[:, b0:b0 + BW] for _k in dests], S.idin)
        if core in relays:
            dests = relays[core][1]
            g.wait_ge(S.rin, _bits(_mask(T, topo, cores[i], [core], True)))
            n += _send(g, T, topo, core, T.relay[:, :], [cores[k] for k in dests],
                       [land[:, _slot(order, k, i), C_HI:SLOT] for k in dests], S["f%d" % i])
        g.wait_ge(S.sent, n)
        return

    rank = T.rank_of(core)
    if rank is None:
        return
    v, a, pe, sy = g.vector, g.scalar, g.tensor, g.sync
    pool = [0]

    def sem():
        pool[0] += 1
        return S["c%d" % (pool[0] - 1)]

    early, late = order[rank]
    others = early + late
    NE = _bits(topo.mask(core, cores[others[0]]))

    def arr(i):
        return (S["f%d" % i], NE)

    sy.dma_start(T.x[0:64, 8:10], T.ml[:, :]).then_inc(S.ldml, 16)
    a.dma_start(T.x[64:128, 8:10], T.ml[:, :]).then_inc(S.ldml, 16)
    sy.dma_start(land[0:64, 0, C_O:SLOT], T.o[:, 0:64]).then_inc(S.ldo, 16)
    a.dma_start(land[64:128, 0, C_O:SLOT], T.o[:, 64:128]).then_inc(S.ldo, 16)
    base = BW * len(late)
    nsent = 0
    v.memset(T.ones[:, 0:(BW if helpers[rank] else 128 - base)], 1.0).then_inc(S.ones, 1)
    v.memset(T.zc[:, 0:1], 0.0).then_inc(S.zc, 1)
    v.memset(T.x[:, 0:1], BIG).then_inc(S.cst, 1)
    v.memset(T.x[:, 4:5], -BIG).then_inc(S.cst, 1)
    v.memset(T.yc[:, 0:1], 1.0).then_inc(S.cst, 1)
    v.memset(T.yc[:, 1:2], -1.0).then_inc(S.cst, 1)
    v.memset(T.yc[:, 2:3], 1.0).then_inc(S.cst, 1)
    g.wait_ge(S.ones, 1)
    if helpers[rank]:
        b0 = _blkcol(order, carry, carriers, rank)
        g.affine_select(T.blk[:, :], T.ones[:, 0:BW], [[-1, BW]], AluOpType.is_equal, 0.0, -b0, 1).then_inc(S.blk, 1)
        g.wait_ge(S.blk, 1)
        nsent += _send(g, T, topo, core, T.blk[:, :], carriers[rank], [T.blk[:, :] for _h in carriers[rank]], S.bin, True)
    else:
        g.affine_select(T.ident[:, base:128], T.ones[:, 0:128 - base], [[-1, 128 - base]], AluOpType.is_equal, 0.0,
                        -base, 1).then_inc(S.ident, 1)
    z2 = sem()
    a.wait_ge(S.zc, 1)
    a.activation(T.f0[:, 0:1], T.zc[:, 0:1], EXP).then_inc(z2, 1)

    pb, pc = sem(), sem()
    v.wait_ge(S.cst, 5)
    v.wait_ge(S.ldml, 32)
    v.tensor_tensor_scan(land[:, 0, C_HI - 1:C_LO + 1], T.x[:, 0:12:4], T.yc[:, 0:3], T.x[:, 8:9], ADD, MUL).then_inc(pc, 1)
    v.tensor_copy(land[:, 0, C_L:C_L + 1], T.x[:, 9:10]).then_inc(pb, 1)

    g.wait_ge(S.ldo, 32)
    g.wait_ge(pb, 1)
    g.wait_ge(pc, 1)
    src = land[:, 0, C_HI:SLOT]
    if helpers[rank]:
        nsent += _send(g, T, topo, core, src, helpers[rank], [T.relay[:, :] for _h in helpers[rank]], S.rin, True)
    if direct[rank]:
        nsent += _send(g, T, topo, core, src, [cores[k] for k in direct[rank]],
                       [land[:, _slot(order, k, rank), C_HI:SLOT] for k in direct[rank]], S["f%d" % rank])

    z1, z3 = sem(), sem()
    v.wait_ge(pc, 1)
    v.tensor_tensor(T.nm[:, 0:1], land[:, 0, C_HI:C_HI + 1], land[:, 0, C_LO:C_LO + 1], SUB).then_inc(z1, 1)
    v.wait_ge(z2, 1)
    v.wait_ge(S.ldo, 32)
    v.wait_ge(pb, 1)
    v.tensor_scalar(T.part[:, :], land[:, 0, C_L:SLOT], T.f0[:, 0:1], None, MUL).then_inc(z3, 1)
    v.wait_ge(z1, 1)
    v.wait_ge(z3, 1)
    a.wait_ge(z1, 1)
    nid = sum(_bits(_mask(T, topo, h, [core])) for h in makers[rank])
    for i in late:
        nid += sum(_bits(_mask(T, topo, c, [core])) for c in carriers[i] if rank in carry[c][1])
    if nid:
        pe.wait_ge(S.idin, nid)
    if not helpers[rank]:
        pe.wait_ge(S.ident, 1)

    ratio = len(late) == 1 and len(early) >= 1
    now = early if ratio else others
    k = 1 + len(now)
    ps = T.ps[:, 0:65]
    s5, s6, s7 = sem(), sem(), sem()
    for i in now:
        v.wait_ge(*arr(i))
        a.wait_ge(*arr(i))
    v.tensor_reduce(T.na[:, 0:1], land[:, 0:k, C_HI], AxisListType.X, MIN).then_inc(s6, 1)
    v.tensor_tensor(T.nm[:, 1:k], land[:, 1:k, C_HI], land[:, 1:k, C_LO], SUB).then_inc(s5, 1)
    s6b = sem()
    if ratio:
        v.wait_ge(s6, 1)
        v.tensor_scalar(T.nc[:, 0:1], T.na[:, 0:1], -60.0, None, ADD).then_inc(s6b, 1)
    a.wait_ge(s5, 1)
    a.wait_ge(s6, 1)
    a.activation(T.f1[:, 0:k], T.nm[:, 0:k], EXP, bias=T.na[:, 0:1], scale=-1.0).then_inc(s7, 1)
    v.wait_ge(s7, 1)
    a.wait_ge(s7, 1)
    ds = []
    for e in range(k):
        d = sem()
        ds.append(d)
        x = T.part[:, :] if e == 0 else land[:, e, C_L:SLOT]
        if (e % 2 == 0) if ratio else (e == 0):
            v.tensor_scalar(T.sc[:, e, 0:65], x, T.f1[:, e:e + 1], None, MUL).then_inc(d, 1)
        else:
            a.activation(T.sc[:, e, 0:65], x, COPY, scale=T.f1[:, e:e + 1]).then_inc(d, 1)
    mm = None
    md = None
    for e in range(k):
        pe.wait_ge(ds[e], 1)
        mm = pe.matmul(ps, T.ident[:, :], T.sc[:, e, 0:65], e == 0, (not ratio) and e == k - 1)
        if ratio:
            md = pe.matmul(T.psd[:, 0:1], T.ident[:, :], T.sc[:, e, 0:1], e == 0, e == k - 1)

    m2, s11, s12 = sem(), sem(), sem()
    if ratio:
        s8, s9, s10, sd, sn = sem(), sem(), sem(), sem(), sem()
        md.then_inc(sd, 1)
        v.wait_ge(s6b, 1)
        v.wait_ge(*arr(late[0]))
        v.tensor_scalar(T.wc[:, 0:1], land[:, k, C_HI:C_HI + 1], land[:, k, C_LO:C_LO + 1], T.nc[:, 0:1],
                        SUB, MAX).then_inc(s8, 1)
        a.wait_ge(*arr(late[0]))
        a.wait_ge(s8, 1)
        a.activation(T.cc[:, 0:1], T.wc[:, 0:1], EXP, bias=T.na[:, 0:1], scale=-1.0).then_inc(s9, 1)
        a.wait_ge(s9, 1)
        a.activation(T.sc[:, k, 0:65], land[:, k, C_L:SLOT], COPY, scale=T.cc[:, 0:1]).then_inc(s10, 1)
        pe.wait_ge(s10, 1)
        mm = pe.matmul(ps, T.ident[:, :], T.sc[:, k, 0:65], False, True)
        v.wait_ge(s9, 1)
        v.wait_ge(sd, 1)
        v.tensor_scalar(T.dn[:, 0:1], land[:, k, C_L:C_L + 1], T.cc[:, 0:1], T.psd[:, 0:1], MUL, ADD).then_inc(sn, 1)
        v.wait_ge(sn, 1)
        v.reciprocal(T.rc[:, 0:1], T.dn[:, 0:1]).then_inc(s11, 1)
        mm.then_inc(m2, 1)
        v.wait_ge(m2, 1)
    else:
        sa, sb = sem(), sem()
        v.tensor_tensor(T.fl[:, 0:k], T.f1[:, 0:k], land[:, 0:k, C_L], MUL).then_inc(sa, 1)
        v.wait_ge(sa, 1)
        v.tensor_reduce(T.dn[:, 0:1], T.fl[:, 0:k], AxisListType.X, ADD).then_inc(sb, 1)
        v.wait_ge(sb, 1)
        v.reciprocal(T.rc[:, 0:1], T.dn[:, 0:1]).then_inc(s11, 1)
        mm.then_inc(m2, 1)
        v.wait_ge(m2, 1)

    v.wait_ge(s11, 1)
    v.tensor_scalar(T.ysb[:, :], T.ps[:, 1:65], T.rc[:, 0:1], None, MUL).then_inc(s12, 1)
    sy.wait_ge(s12, 1)
    sy.dma_start(T.y[:, 0:64], T.ysb[0:64, :]).then_inc(S.st, 16)
    a.wait_ge(s12, 1)
    a.dma_start(T.y[:, 64:128], T.ysb[64:128, :]).then_inc(S.st, 16)
    g.wait_ge(S.sent, nsent)
    g.wait_ge(S.st, 32)
